import numpy as np, ml_dtypes
CORES = [2,3,42,43,82,83,122,123]
N = 8
BF = ml_dtypes.bfloat16
def gentries(a):
    return np.ascontiguousarray(a.reshape(8, 16, -1).transpose(0, 2, 1)).reshape(8, -1)
def gtable(e):
    e = np.asarray(e); return np.ascontiguousarray(e.reshape(8, -1, 16).transpose(0, 2, 1)).reshape(128, -1).astype(np.int32)
W, M, B, T, P, QU, TH = 4096, 512, 192, 5, 1, 11, 254
def parts(rng):
    d = {}
    d["pr"] = (224 * rng.random((N, 8, 1, W)) ** 3 + 32 * rng.random((N, 8, 16, W))).astype(np.int64)
    d["ad"] = (np.exp2(rng.integers(2, 8, (N, 8, 1, W))) * rng.random((N, 8, 16, W))).astype(np.int64)
    d["mc"] = rng.integers(0, W, (N, 8, 16, M))
    d["gl"] = (224 * rng.random((N, 8, 1, M)) + 32 * rng.random((N, 8, 16, M))).astype(np.int64)
    d["z"] = (224 * rng.random((N, 8, 1, B)) + 32 * rng.random((N, 8, 16, B))).astype(np.int64)
    d["m"] = rng.integers(0, M, (N, 8, B))
    d["dv"] = (np.exp2(rng.integers(2, 8, (N, 8, 1, T * P))) * rng.random((N, 8, 16, T * P))).astype(np.int64)
    d["wt"] = rng.integers(0, 256, (N, 8, 16, 1))
    return d
def flat(a):
    return np.ascontiguousarray(np.reshape(a, (N, 128, -1)))
def pack(d):
    h = {k: flat(d[k]).astype(np.float32).astype(BF) for k in ("pr", "ad", "gl", "z", "dv", "wt")}
    return {"pr": h["pr"], "ad": h["ad"], "mc": flat(d["mc"]).astype(np.int32), "gl": h["gl"], "z0": h["z"], "m0": np.stack([gtable(a) for a in d["m"]]), "dv": h["dv"], "wt": h["wt"]}
def setup_inputs(rng):
    return pack(parts(rng))
def sized(rng, hi, *shape):
    return np.minimum((float(hi + 1) ** rng.random(shape[:-2] + (1, shape[-1])) * rng.random(shape)).astype(np.int64), hi)
def setup_inputs_spread(rng):
    d = parts(rng)
    d["pr"] = sized(rng, 255, N, 8, 16, W); d["ad"] = sized(rng, 127, N, 8, 16, W); d["dv"] = sized(rng, 255, N, 8, 16, T * P); d["wt"] = sized(rng, 255, N, 8, 16, 1)
    a = sized(rng, 255, N, 8, 16, M); d["gl"] = np.where(rng.random((N, 8, 1, M)) < 0.5, 255 - a, a)
    a = sized(rng, 255, N, 8, 16, B); d["z"] = np.where(rng.random((N, 8, 1, B)) < 0.6, rng.integers(0, 256, (N, 8, 16, B)), a)
    d["mc"] = np.minimum((W * rng.random((N, 8, 16, M)) ** 3).astype(np.int64), W - 1)
    d["m"] = np.minimum((M * rng.random((N, 8, B)) ** 2).astype(np.int64), M - 1)
    return pack(d)
def mix(rng, hi, *shape):
    q = rng.choice(np.array([0.0, 0.1, 0.5, 0.8, 0.9, 1.0]), shape[:-2] + (1, shape[-1]))
    return (rng.random(shape) < q).astype(np.int64) * hi
def setup_inputs_ends(rng):
    d = {"pr": mix(rng, 255, N, 8, 16, W), "ad": mix(rng, 127, N, 8, 16, W), "mc": mix(rng, W - 1, N, 8, 16, M), "gl": mix(rng, 255, N, 8, 16, M), "z": mix(rng, 255, N, 8, 16, B),
         "m": (M - 1) * rng.integers(0, 2, (N, 8, B)), "dv": mix(rng, 255, N, 8, 16, T * P), "wt": mix(rng, 255, N, 8, 16, 1)}
    pr, ad, mc, gl, z, m, dv, wt = [d[k] for k in ("pr", "ad", "mc", "gl", "z", "m", "dv", "wt")]; a = N - 1
    wt[:, 0, :8] = 0; wt[:, 0, 8:] = 255
    gl[0, :, :, 0] = 0; gl[0, :, :, M - 1] = 0
    gl[1, :, :, 0] = 0; gl[1, :, :, M - 1] = 255; m[1] = 0; m[1, 7, B - 1] = M - 1; z[1, 7, :, B - 1] = 0; dv[1, 7, :, :P] = 0
    pr[a, 7, :, 0] = 255; ad[a, 7, :, 0] = 127; ad[a, 7, :, W - 1] = 0; gl[a, 7, :, 0] = 255; gl[a, 7, :, M - 1] = 255
    mc[a, 7, :, 0] = 0; mc[a, 7, :, M - 1] = W - 1
    wt[a, 7] = 0; wt[a, 7, 15] = 255; wt[a, 7, 13:15] = 1
    for i in (0, 1, B - 2, B - 1): z[a, 7, :, i] = 255
    m[a, 7, 1] = 0; m[a, 7, B - 2] = 0; m[a, 7, B - 1] = M - 1
    m[a, 7, :B - 1] = np.where(np.all(z[a, 7, 13:, :B - 1] == 255, axis=0), 0, m[a, 7, :B - 1])
    wt[a, 6] = 255; gl[a, 6, :, 0] = 0; z[a, 6, :, 0] = 255; z[a, 6, :, B - 1] = 255; z[a, 6, :, 1] = 0; z[a, 6, :, B - 2] = 0
    m[a, 6, 0] = 0; m[a, 6, 1] = 0; m[a, 6, B - 2] = 0; m[a, 6, B - 1] = M - 1
    return pack(d)
def setup_inputs_corners(rng):
    d = parts(rng); pr, ad, mc, gl, z, m, dv, wt = [d[k] for k in ("pr", "ad", "mc", "gl", "z", "m", "dv", "wt")]
    m[:, 0] = 0; m[:, 1] = M - 1; m[:, 2] = np.arange(B); m[:, 3] = M - 1 - np.arange(B)
    wt[:, 0] = 0; wt[:, 1] = 255; dv[:, 4] = 255; dv[:, 5] = 0
    one = rng.integers(0, W, (N, 1, M)); one[:, 0, 0] = 0; one[:, 0, M - 1] = W - 1; mc[:, 4] = one; m[:, 4, 0] = 0; m[:, 4, B - 1] = M - 1
    gl[:, 5] = np.maximum(gl[:, 5], 1); goal = np.take_along_axis(gl[:, 5], m[:, 5][:, None, :], 2)
    c = rng.choice(np.array([0, QU - 1, QU, QU + 1, 16]), (N, 1, B)); place = np.argsort(np.argsort(rng.random((N, 16, B)), axis=1), axis=1)
    z[:, 5] = goal - (place >= c)
    ad[:, 6] = TH // 16; ad[:, 6, 15] = TH - 15 * (TH // 16) + rng.integers(-1, 2, (N, W))
    pr[:, 6] = np.maximum(pr[:, 6], 40); gl[:, 6] = np.maximum(gl[:, 6], 200); z[:, 6] = np.where(rng.random((N, 1, B)) < 0.7, 255, z[:, 6])
    pr[:, 7] = 255; gl[:, 7] = 255; z[:, 7] = 255 * rng.integers(0, 2, (N, 1, B)); wt[:, 7] = (255 * (np.arange(N) & 1)).reshape(N, 1, 1)
    return pack(d)
def setup_inputs_crowd(rng):
    d = parts(rng); pr, gl, z, m, dv, wt = [d[k] for k in ("pr", "gl", "z", "m", "dv", "wt")]
    gl[:, :6] = 0; m[:, :4] = np.argsort(rng.random((N, 4, M)), axis=-1)[..., :B]
    wt[:, :4] = 0; wt[:, :4, 0] = 1; wt[:, :4, 1] = 255
    c = np.full((N, 4, B), M - 1); c[:, 1, 0] = 0; c[:, 3] = rng.choice(np.array([0, 1, M // 2, M - 1]), (N, B))
    v = (c - 37 * m[:, :4]) & (M - 1); z[:, :4, 0] = v - 255 * (v // 255); z[:, :4, 1] = v // 255
    for i in range(N): gl[i, 2, :, m[i, 2, 0]] = 255
    z[:, 2, 2:, 0] = 100; dv[:, 2, :, :P] = 1
    for g in (4, 5):
        z[:, g] = z[:, g, :, :1].copy(); m[:, g] = m[:, g, :1].copy()
    z[:, 5, :, B - 1] = 255 - z[:, 5, :, 0]
    gl[:, 6] = 255
    pr[:, 7] = 255; gl[:, 7] = 255; z[:, 7] = 0; z[:, 7, :, B - 1] = 255; m[:, 7] = m[:, 7, :1].copy()
    return pack(d)
def setup_inputs_few(rng):
    d = parts(rng); d["z"] = np.minimum(d["z"], 254); d["dv"] = np.maximum(d["dv"], 1)
    mc, gl, z, m, wt = [d[k] for k in ("mc", "gl", "z", "m", "wt")]
    gl[1::2] = 255; z[1::2, 7, :, B - 1] = 255
    full = rng.permutation(np.array([0, 1, 3, 4]))
    for i in range(0, N, 2):
        g = int(full[(i // 2) & 3]); gl[i, g] = 0; m[i, g] = rng.permutation(M)[:B]
        wt[i, g] = 0; wt[i, g, 0] = 1; wt[i, g, 1] = 255
        a = rng.choice(np.array([11, 13, 23, 25, 27, 29]), B); u = W - 32 + a
        z[i, g, 1] = u // 255; z[i, g, 0] = u - 255 * (u // 255)
        mc[i, g, 15, m[i, g]] = W - 32 + ((-(a ** 7)) & 31)
    return pack(d)
def check_inputs(d):
    bad = []
    for k, hi in (("pr", 255), ("ad", 127), ("mc", W - 1), ("gl", 255), ("z0", 255), ("m0", M - 1), ("dv", 255), ("wt", 255)):
        a = np.asarray(d[k]).astype(np.float64)
        if not (np.min(a) >= 0 and np.max(a) <= hi): bad.append("range of " + k)
        elif np.any(a != np.floor(a)): bad.append("whole numbers of " + k)
    return bad
def reference(pr, ad, mc, gl, z0, m0, dv, wt):
    need_of, add_of, goal_of, z, dist, weight = [a.astype(np.float32).astype(np.int64).reshape(N, 8, 16, -1) for a in (pr, ad, gl, z0, dv, wt)]
    tb = mc.astype(np.int64).reshape(N, 8, 16, M); m = np.stack([gentries(a) for a in m0]).astype(np.int64)
    seen = [0] * N
    for t in range(T):
        for q in range(N):
            s = (q - t) % N; zz = z[s]; mm = m[s]
            o = np.take_along_axis(tb[q], mm[:, None, :], 2)
            ix = o.reshape(8, 1, 16 * B)
            p = np.take_along_axis(need_of[q], ix, 2).reshape(8, 16, 16, B); a = np.take_along_axis(add_of[q], ix, 2).reshape(8, 16, 16, B)
            K = [None] * 16 + [np.take_along_axis(goal_of[q], mm[:, None, :], 2)]
            for k in range(15, -1, -1): K[k] = np.maximum(p[:, :, k], K[k + 1] - a[:, :, k])
            K = np.stack(K)
            for j in range(P):
                met = np.add.reduce((zz[None] >= K).astype(np.int64), axis=2)
                best = np.max(np.where(met >= QU + (seen[q] & 1), np.arange(17).reshape(17, 1, 1), -1), axis=0)
                ak = np.take_along_axis(a, np.clip(best, 0, 15)[:, None, None, :], 2)[:, :, 0]
                new = np.abs(np.minimum(255, zz + ak) - dist[q, :, :, t * P + j][:, :, None])
                zz = np.where(((best >= 0) & (best < 16))[:, None, :], new, zz)
            goal = best == 16
            u = np.add.reduce(weight[q] * zz, axis=1) & (W - 1); to = (u + 37 * mm) & (M - 1)
            use = np.add.reduce(np.minimum(a, K[1:].transpose(1, 2, 0, 3)), axis=1)
            fresh = (((o * u[:, None, :]) >> 5) + o + 37 * np.arange(16).reshape(1, 16, 1)) & (W - 1)
            o = np.where(use < TH, fresh, o)
            for g in range(8):
                who = np.flatnonzero(goal[g]); where, first = np.unique(to[g, who], return_index=True)
                tb[q, g][:, where] = o[g][:, who[first]]
            z[s] = zz; m[s] = np.where(goal | (best < 0), to, mm); seen[q] = int(np.count_nonzero(goal))
    back = [(q - (T - 1)) % N for q in range(N)]
    return {"ymc": tb.reshape(N, 128, M).astype(np.float32), "yz": z[back].reshape(N, 128, B).astype(np.float32), "ym": np.stack([gtable(m[s]) for s in back]).astype(np.float32)}

@@ -1,0 +1,448 @@
+from concourse.mybir import dt, AluOpType, AxisListType, ActivationFunctionType
+
+A = AluOpType
+AF = ActivationFunctionType
+STEPS = 5
+B16 = "bfloat16"
+F32 = "float32"
+F16 = "float16"
+I32 = "int32"
+U16 = "uint16"
+BANKS = ["p%d" % b for b in range(8)]
+SCRATCH = {}
+for _names, _cols, _type in (
+        ("prw adw", 4096, B16), ("glw imw", 512, B16), ("mci", 512, I32), ("mcf yms", 512, F32), ("tb", 704, F32),
+        ("mi", 12, I32), ("dvs", 5, B16), ("wts", 1, B16),
+        ("d0 d1 ss", 6144, B16), ("ind", 3072, B16), ("ol", 192, U16), ("gg mb na15 r15 gi indk oh zdb xx wn", 192, B16),
+        ("zt", 256, B16), ("tg", 384, F16), ("ui ua", 384, I32), ("tgs", 24, F32), ("mlf kl tol ya yb mn", 12, F32),
+        ("acc", 1, F32), ("ai ai2", 1, I32), ("thr", 8, F32), ("si", 192, F16), ("sl la", 12, U16),
+        ("yy yzs of fd fw", 192, F32), ("f1 f2 f3 f4", 192, I32),
+        ("pi kki gri", 1, I32), ("pf kkf grf k37 kw jc jt", 1, F32), ("iw", 192, F32), ("ig cj onf", 128, F32), ("ie ce", 1536, B16),
+        ("cid cidn c296 cb cbh tma tmb ctm cg4 cnb wb wb8", 128, B16), ("sel selk seln", 2048, B16), ("dg dd", 640, B16),
+        ("ic bl", 12, F32), ("b32 one12", 12, B16), ("b512", 12, F16), ("ns", 192, F16), ("c255", 192, B16)):
+    for _n in _names.split():
+        SCRATCH[_n] = ("sbuf", [128, _cols], _type)
+SCRATCH["eb"] = ("sbuf", [128, 12, 208], B16)
+SCRATCH["mk"] = ("sbuf", [128, 12, 16], B16)
+for _t in range(STEPS):
+    SCRATCH["zb%d" % _t] = ("sbuf", [128, 192], B16)
+    SCRATCH["ml%d" % _t] = ("sbuf", [128, 12], U16)
+    if _t:
+        SCRATCH["zs%d" % _t] = ("sbuf", [128, 192], B16)
+        SCRATCH["ms%d" % _t] = ("sbuf", [128, 12], U16)
+for _b in BANKS:
+    SCRATCH[_b] = ("psum", [128, 512], F32)
+LOADS = ["mc", "m0", "z0", "ad", "gl", "pr", "wt", "dv"]
+SEMAPHORES = ["cv", "cs", "ct", "cg", "outz", "outm", "outa", "outb", "snd"] + ["ld_" + n for n in LOADS]
+SEMAPHORES += ["mr%d" % t for t in range(1, STEPS)] + ["zr%d" % t for t in range(1, STEPS)]
+
+
+def scheduler(g, T):
+    queues = {"g": g, "v": g.vector, "s": g.scalar, "t": g.tensor, "y": g.sync}
+    ops = []
+    wr, rd, bank = {}, {}, {}
+
+    def op(q, fn, r=(), w=(), ext=None):
+        i = len(ops)
+        deps = set()
+        for x in list(r) + list(w):
+            if x in BANKS:
+                h = bank.setdefault(x, {})
+                deps.update(h[k] for k in h if k != q or (q != "t" and x in w))
+                h[q] = i
+        for x in r:
+            if x not in BANKS:
+                if x in wr:
+                    deps.add(wr[x])
+                rd.setdefault(x, {})[q] = i
+        for x in w:
+            if x not in BANKS:
+                if x in wr:
+                    deps.add(wr[x])
+                deps.update(rd.get(x, {}).values())
+                wr[x] = i
+                rd[x] = {}
+        deps.discard(i)
+        ops.append({"q": q, "fn": fn, "deps": deps, "ext": ext})
+
+    def emit():
+        pos, known, snap, need, waits = {}, {}, [], set(), []
+        for i, o in enumerate(ops):
+            q = o["q"]
+            pos[q] = pos.get(q, 0) + 1
+            o["pos"] = pos[q]
+            k = known.setdefault(q, {})
+            mine = []
+            for d in sorted(o["deps"], reverse=True):
+                e = ops[d]["ext"]
+                key, val = (e[0], e[1]) if e else (ops[d]["q"], ops[d]["pos"])
+                if k.get(key, 0) >= val:
+                    continue
+                mine.append(d)
+                need.add(d)
+                for a, b in snap[d].items():
+                    k[a] = max(k.get(a, 0), b)
+                k[key] = max(k.get(key, 0), val)
+            waits.append(mine)
+            snap.append(dict(k))
+        last = {}
+        for i, o in enumerate(ops):
+            if not o["ext"]:
+                last[o["q"]] = i
+        need.update(last.values())
+        count = {}
+        for i, o in enumerate(ops):
+            if i in need and not o["ext"]:
+                count[o["q"]] = count.get(o["q"], 0) + 1
+                o["tok"] = ("c" + o["q"], count[o["q"]])
+        for i, o in enumerate(ops):
+            if o["fn"] is None:
+                continue
+            Q = queues[o["q"]]
+            best = {}
+            for d in waits[i]:
+                s, n = (ops[d]["ext"] or ops[d]["tok"])[:2]
+                best[s] = max(best.get(s, 0), n)
+            for s, n in best.items():
+                Q.wait_ge(T.sem[s], n)
+            ins = o["fn"](Q)
+            if o["ext"]:
+                if o["ext"][2]:
+                    ins.then_inc(T.sem[o["ext"][0]], 16)
+            elif i in need:
+                ins.then_inc(T.sem["c" + o["q"]], 1)
+        for q, n in count.items():
+            g.wait_ge(T.sem["c" + q], n)
+
+    return op, emit
+
+
+def regs(name, a, b):
+    return ["%s.%d" % (name, c) for c in range(a, b)]
+
+
+def rank_program(g, core, T, topo):
+    rank = T.rank_of(core)
+    if rank is None:
+        return
+    op, emit = scheduler(g, T)
+    n_ranks = len(T.cores)
+    nxt = T.cores[(rank + 1) % n_ranks]
+    n_eng = 8
+    mask_out = sum(1 << e for e in topo.engines(core, nxt)[:n_eng])
+    rid, pid = topo.addr(nxt)[:2]
+
+    def V(fn, r=(), w=()):
+        op("v", fn, r, w)
+
+    def S(fn, r=(), w=()):
+        op("s", fn, r, w)
+
+    def P(fn, r=(), w=()):
+        op("t", fn, r, w)
+
+    def G(fn, r=(), w=()):
+        op("g", fn, r, w)
+
+    def ts(out, in0, s1, s2, *o):
+        return lambda Q: Q.tensor_scalar(out, in0, s1, s2, *o)
+
+    def tt(out, a, b, o):
+        return lambda Q: Q.tensor_tensor(out, a, b, o)
+
+    def cp(out, a):
+        return lambda Q: Q.tensor_copy(out, a)
+
+    def act(out, a, f, **k):
+        return lambda Q: Q.activation(out, a, f, **k)
+
+    def ms(out, c):
+        return lambda Q: Q.memset(out, c)
+
+    def mm(out, a, b, start=True, stop=True):
+        return lambda Q: Q.matmul(out, a, b, start, stop)
+
+    def iota(out, pattern, base=0, cm=0):
+        return lambda Q: Q.iota(out, pattern, base, cm, allow_small_or_imprecise_dtypes=True)
+
+    def load(q, name, buf):
+        op(q, lambda Q: Q.dma_start(T[buf][:], T[name][:]), [], [buf], ("ld_" + name, 16, True))
+
+    load("y", "mc", "mci")
+    load("s", "m0", "mi")
+    load("y", "ad", "adw")
+    load("s", "pr", "prw")
+    load("y", "gl", "glw")
+    load("y", "z0", "zb0")
+    load("y", "wt", "wts")
+    load("y", "dv", "dvs")
+
+    G(lambda Q: Q.iota(T.pi[:], [[0, 1]], 0, 1), [], ["pi"])
+    G(iota(T.ig[:], [[1, 8], [0, 16]]), [], ["ig"])
+    G(iota(T.iw[:], [[1, 192]]), [], ["iw"])
+    G(iota(T.ie[:], [[1, 96], [0, 16]]), [], ["ie"])
+    G(iota(T.ic[:], [[16, 12]]), [], ["ic"])
+    G(iota(T.imw[:, 0:256], [[1, 256]]), [], ["imwa"])
+    G(iota(T.imw[:, 256:512], [[1, 256]], -256), [], ["imwb"])
+    V(ms(T.d0[:, 1::2], 0.0), [], ["d0z"])
+    V(ms(T.sel[:], 0.0), [], ["selz"])
+    V(ts(T.kki[:], T.pi[:], 15, None, A.bitwise_and), ["pi"], ["kki"])
+    V(ts(T.gri[:], T.pi[:], 4, None, A.arith_shift_right), ["pi"], ["gri"])
+    V(cp(T.pf[:], T.pi[:]), ["pi"], ["pf"])
+    V(cp(T.kkf[:], T.kki[:]), ["kki"], ["kkf"])
+    V(cp(T.grf[:], T.gri[:]), ["gri"], ["grf"])
+    V(ts(T.kw[:], T.kkf[:], 2.0, -1.0, A.mult, A.add), ["kkf"], ["kw"])
+    V(ts(T.cb[:], T.ig[:], T.grf[:], None, A.is_equal), ["ig", "grf"], ["cb"])
+    for i in range(16):
+        V(cp(T.sel[:, 129 * i:129 * i + 113:16], T.cb[:, 0::16]), ["cb", "selz"], ["sel"] if i == 15 else [])
+    S(act(T.d1[:, 0::2], T.d0[:, 1::2], AF.Copy), ["d0z"], ["d1z"])
+    S(act(T.seln[:], T.sel[:], AF.Copy, scale=-1.0), ["sel"], ["seln"])
+    S(act(T.selk[:], T.sel[:], AF.Copy, scale=T.kw[:]), ["sel", "kw"], ["selk"])
+    V(ts(T.k37[:], T.kkf[:], -37.0, 555.0, A.mult, A.add), ["kkf"], ["k37"])
+    V(tt(T.jt[:], T.pf[:], T.kw[:], A.subtract), ["pf", "kw"], ["jt"])
+    V(ts(T.jc[:], T.jt[:], 14.0, None, A.add), ["jt"], ["jc"])
+    V(ts(T.cj[:], T.iw[:, 0:128], T.jc[:], None, A.is_equal), ["iw", "jc"], ["cj"])
+    V(cp(T.mcf[:], T.mci[:]), ["mci"], ["mcf"])
+    P(mm(T.p0[:], T.cj[:], T.mcf[:]), ["cj", "mcf"], ["p0"])
+    V(cp(T.ml0[:], T.mi[:]), ["mi"], ["ml0"])
+    V(ts(T.cid[:], T.iw[:, 0:128], T.pf[:], None, A.is_equal), ["iw", "pf"], ["cid"])
+    V(cp(T.tb[:, 0:512], T.p0[:]), ["p0"], ["tb"])
+
+    def consts():
+        V(ts(T.ce[:], T.ie[:], T.pf[:], None, A.is_equal), ["ie", "pf"], ["ce"])
+        V(ts(T.cidn[:], T.cid[:], -1.0, None, A.mult), ["cid"], ["cidn"])
+        V(ts(T.c296[:], T.cid[:], 296.0, None, A.mult), ["cid"], ["c296"])
+        V(ts(T.cg4[:], T.cb[:], -4.0, None, A.mult), ["cb"], ["cg4"])
+        V(ts(T.cbh[:], T.cb[:], 0.5, None, A.mult), ["cb"], ["cbh"])
+        V(ts(T.cnb[:], T.cb[:], -16.0, None, A.mult), ["cb"], ["cnb"])
+        V(ms(T.thr[:], 11.0), [], ["thr0"])
+        for c in range(12):
+            V(ts(T.mk[:, c, :], T.iw[:, 0:16], T.kkf[:], None, A.is_gt), ["iw", "kkf"], ["mk"] if c == 11 else [])
+        V(ts(T.tma[:], T.iw[:, 0:128], T.pf[:], 2.0, A.is_gt, A.mult), ["iw", "pf"], ["tma"])
+        V(tt(T.tmb[:], T.tma[:], T.cb[:], A.mult), ["tma", "cb"], ["tmb"])
+        V(tt(T.ctm[:], T.tmb[:], T.cid[:], A.subtract), ["tmb", "cid"], ["ctm"])
+        V(ts(T.bl[:], T.ic[:], T.kkf[:], None, A.add), ["ic", "kkf"], ["bl"])
+        V(ts(T.b32[:], T.bl[:], 32.0, None, A.mult), ["bl"], ["b32"])
+        V(ts(T.b512[:], T.bl[:], 512.0, 16.0, A.add, A.mult), ["bl"], ["b512"])
+        V(ms(T.one12[:], 1.0), [], ["one12"])
+        V(ts(T.ns[:], T.iw[:], -1.0, -513.0, A.mult, A.add), ["iw"], ["ns"])
+        V(ms(T.c255[:], -15.9375), [], ["c255"])
+        V(ms(T.onf[:], 1.0), [], ["onf"])
+        V(ts(T.wb[:], T.cb[:], T.wts[:], None, A.mult), ["cb", "wts"], ["wb"])
+        V(ts(T.wb8[:], T.cb[:], T.wts[:], 8.0, A.mult, A.mult), ["cb", "wts"], ["wb8"])
+        for t in range(STEPS):
+            V(ts(T.dg[:, 128 * t:128 * t + 128], T.cid[:], T.dvs[:, t:t + 1], None, A.mult), ["cid", "dvs"], ["dg%d" % t])
+
+    def distances():
+        for t in range(STEPS):
+            P(mm(T.p2[:, 128 * (t % 4):128 * (t % 4) + 128], T.cb[:], T.dg[:, 128 * t:128 * t + 128]), ["cb", "dg%d" % t], ["p2"])
+            if t == 3:
+                S(act(T.dd[:, 0:512], T.p2[:], AF.Copy), ["p2"], ["dda"])
+        S(act(T.dd[:, 512:640], T.p2[:, 0:128], AF.Copy), ["p2"], ["ddb"])
+
+    def listmm(pb, col, width, mats, buf, total, base=(), names=None):
+        def fn(Q):
+            out = T[pb][:, col:col + width]
+            first = True
+            for b in base:
+                Q.matmul(out, T.cid[:], T[b][:], first, False)
+                first = False
+            for i in range(16):
+                ins = Q.matmul(out, T[mats][:, 128 * i:128 * i + 128], T[buf][:, i:total:16], first, i == 15)
+                first = False
+            return ins
+        P(fn, ["cid", mats] + (names or [buf]) + list(base), [pb])
+
+    def step(t):
+        lastt = t == STEPS - 1
+        ml, z, th = "ml%d" % t, "zb%d" % t, "thr%d" % t
+        if t:
+            op(None, None, [], [ml], ("mr%d" % t, n_eng, False))
+            op(None, None, [], [z], ("zr%d" % t, n_eng, False))
+
+        def na(a, b):
+            S(act(T.d0[:, 1024 * a:1024 * b:2], T.adw[:].indirect(T.ol[:, 32 * a:32 * b]), AF.Copy, scale=-1.0), ["adw", "ol"], regs("d0", a, b))
+
+        def pg(q, a, b):
+            out, win = T.d1[:, 1024 * a + 1:1024 * b:2], T.prw[:].indirect(T.ol[:, 32 * a:32 * b])
+            op(q, cp(out, win) if q == "v" else act(out, win, AF.Copy), ["prw", "ol"], regs("d1", a, b))
+
+        def scan(a, b):
+            k = slice(1024 * a, 1024 * b, 32)
+            c = slice(32 * a, 32 * b)
+            V(cp(T.na15[:, c], T.d0[:, k]), regs("d0", a, b), regs("na15", a, b))
+            V(tt(T.d1[:, k], T.gg[:, c], T.d0[:, k], A.add), ["gg"] + regs("d0", a, b), regs("d1", a, b))
+            V(ms(T.d0[:, k], -1024.0), [], regs("d0", a, b))
+            j = slice(1024 * a, 1024 * b)
+            V(lambda Q: Q.tensor_tensor_scan(T.ss[:, j], T.d0[:, j], T.d1[:, j], 0.0, A.add, A.max),
+              ["d0z", "d1z"] + regs("d0", a, b) + regs("d1", a, b), regs("ss", a, b))
+            V(ts(T.r15[:, c], T.d1[:, k], 0.0, None, A.max), regs("d1", a, b), regs("r15", a, b))
+
+        def zexp(c):
+            pb = "p%d" % (c % 2)
+            P(mm(T[pb][:], T.zt[0:96, 128 * (c // 3):128 * (c // 3) + 128], T.ce[0:96, 512 * (c % 3):512 * (c % 3) + 512]), ["zt", "ce"], [pb])
+
+        def cmp(c):
+            pb = "p%d" % (c % 2)
+            V(tt(T.ind[:, 512 * c:512 * c + 512], T.ss[:, 1024 * c + 1:1024 * c + 1024:2], T[pb][:], A.is_le), regs("ss", c, c + 1) + [pb], regs("ind", c, c + 1))
+
+        def cnt(a, b):
+            def fn(Q):
+                out = T.p3[:, 32 * a:32 * b]
+                Q.matmul(out, T.cg4[:], T.tg[:, 192 + 32 * a:192 + 32 * b], True, False)
+                for k in range(16):
+                    ins = Q.matmul(out, T.sel[:, 128 * k:128 * k + 128], T.ind[:, 512 * a + k:512 * b:16], False, k == 15)
+                return ins
+            P(fn, ["sel", "cg4", "tgg"] + regs("ind", a, b), ["p3"])
+
+        def use(a, b):
+            def fn(Q):
+                out = T.p4[:, 32 * a:32 * b]
+                Q.matmul(out, T.sel[:, 0:128], T.gg[:, 32 * a:32 * b], True, False)
+                Q.matmul(out, T.seln[:, 0:128], T.r15[:, 32 * a:32 * b], False, False)
+                for k in range(1, 16):
+                    Q.matmul(out, T.sel[:, 128 * k:128 * k + 128], T.ss[:, 1024 * a + 2 * k - 1:1024 * b:32], False, False)
+                    ins = Q.matmul(out, T.seln[:, 128 * k:128 * k + 128], T.ss[:, 1024 * a + 2 * k:1024 * b:32], False, k == 15)
+                return ins
+            P(fn, ["sel", "seln", "gg"] + regs("r15", a, b) + regs("ss", a, b), ["p4"])
+
+        def dups(a, b):
+            for c in range(a, b):
+                V(ts(T.eb[:, c, 0:192 - 16 * c], T.tg[:, 16 * c:192], T.kl[:, c:c + 1], None, A.is_equal), ["tgt", "kl"], ["eb%d" % c])
+
+        def send(name, src, dst, k):
+            op("g", lambda Q: Q.remote_dma(T[dst][:], T[src][:], T.sem[name], T.sem.snd, pid, rid, mask_out), [src], [], ("snd", n_eng * k, False))
+
+        V(cp(T.ol[:], T.tb[:, 0:512].indirect(T[ml][:])), ["tb", ml], ["ol"])
+        if t == 0:
+            consts()
+        V(cp(T.mlf[:], T[ml][:]), [ml], ["mlf"])
+        na(0, 1)
+        pg("v", 0, 2)
+        P(mm(T.p5[0:96, 0:128], T[z][:, 0:96], T.cid[:]), [z, "cid"], ["p5"])
+        P(mm(T.p5[0:96, 128:256], T[z][:, 96:192], T.cid[:]), [z, "cid"], ["p5"])
+        S(act(T.gg[:], T.glw[:].indirect(T[ml][:]), AF.Copy), ["glw", ml], ["gg"])
+        na(1, 2)
+        P(mm(T.p6[:, 0:192], T.cid[:], T[z][:], True, False), [z, "cid"], ["p6"])
+        P(mm(T.p6[:, 0:192], T.cidn[:], T.gg[:], False, True), ["cidn", "gg"], ["p6"])
+        S(act(T.zt[0:96, :], T.p5[0:96, 0:256], AF.Copy), ["p5"], ["zt"])
+        S(act(T.gi[:], T.p6[:, 0:192], AF.Sign, bias=0.5), ["p6"], ["gi"])
+        S(act(T.mb[:], T.imw[:].indirect(T[ml][:]), AF.Copy), ["imwa", "imwb", ml], ["mb"])
+        na(2, 4)
+        S(act(T.of[:], T.tb[:, 0:512].indirect(T[ml][:]), AF.Copy), ["tb", ml], ["of"])
+        zexp(0)
+        zexp(1)
+        P(mm(T.p5[:, 256:448], T.cbh[:], T.gi[:]), ["cbh", "gi"], ["p5"])
+        P(mm(T.p6[:, 0:192], T.wb[:], T[z][:]), ["wb", z], ["p6"])
+        P(mm(T.p6[:, 192:384], T.wb8[:], T[z][:], True, False), ["wb8", z], ["p6"])
+        P(mm(T.p6[:, 192:384], T.c296[:], T.mb[:], False, True), ["c296", "mb"], ["p6"])
+        scan(0, 1)
+        scan(1, 2)
+        V(ts(T.tg[:, 192:384], T.p5[:, 256:448], 8.0, T.thr[:, t:t + 1], A.add, A.is_ge), ["p5", th], ["tgg"])
+        V(cp(T.ui[:], T.p6[:, 0:384]), ["p6"], ["ui"])
+        V(ts(T.ua[:], T.ui[:], 4095, None, A.bitwise_and), ["ui"], ["ua"])
+        V(ts(T.tg[:, 0:192], T.ua[:, 192:384], 0.125, 1.0, A.mult, A.add), ["ua"], ["tgt"])
+        if t == 0:
+            distances()
+        cmp(0)
+        cmp(1)
+        listmm("p7", 0, 24, "sel", "tg", 384, (), ["tgg", "tgt"])
+        S(act(T.tgs[:, 0:12], T.p7[:, 0:12], AF.Copy, scale=0.0625), ["p7"], ["tgsa"])
+        S(act(T.tgs[:, 12:24], T.p7[:, 12:24], AF.Copy, scale=0.0625, accum_out=T.acc[:]), ["p7"], ["tgsb", "acc"])
+        S(act(T.tol[:], T.p7[:, 0:12], AF.Copy, scale=0.0625, bias=-1.0), ["p7"], ["tol"])
+        if not lastt:
+            P(mm(T.p7[:, 64:65], T.onf[:], T.acc[:]), ["onf", "acc"], ["p7"])
+        S(act(T.p2[:, 0:192], T.of[:], AF.Copy), ["of"], ["p2"])
+        S(act(T.p2[:, 192:384], T.of[:], AF.Identity, bias=T.k37[:]), ["of", "k37"], ["p2"])
+        pg("s", 2, 4)
+        zexp(2)
+        zexp(3)
+        cnt(0, 2)
+        V(tt(T.f1[:], T.ua[:, 0:192], T.p2[:, 0:192], A.mult), ["p2", "ua"], ["f1"])
+        V(ts(T.f2[:], T.f1[:], 5, None, A.arith_shift_right), ["f1"], ["f2"])
+        V(tt(T.kl[:], T.tgs[:, 0:12], T.tgs[:, 12:24], A.mult), ["tgsa", "tgsb"], ["kl"])
+        dups(0, 8)
+        use(0, 2)
+        na(4, 6)
+        pg("s", 4, 5)
+        pg("s", 5, 6)
+        scan(2, 4)
+        cmp(2)
+        cmp(3)
+        zexp(4)
+        zexp(5)
+        P(mm(T.p6[:, 0:192], T.cid[:], T.tg[:, 0:192], True, False), ["cid", "tgt"], ["p6"])
+        P(mm(T.p6[:, 0:192], T.cid[:], T.ns[:], False, True), ["cid", "ns"], ["p6"])
+        cnt(2, 4)
+        V(tt(T.f3[:], T.f2[:], T.p2[:, 192:384], A.add), ["f2", "p2"], ["f3"])
+        V(ts(T.f4[:], T.f3[:], 4095, None, A.bitwise_and), ["f3"], ["f4"])
+        V(tt(T.fd[:], T.f4[:], T.p2[:, 0:192], A.subtract), ["f4", "p2"], ["fd"])
+        use(2, 4)
+        if not lastt:
+            V(cp(T.ai[:], T.p7[:, 64:65]), ["p7"], ["ai"])
+            V(ts(T.ai2[:], T.ai[:], 1, None, A.bitwise_and), ["ai"], ["ai2"])
+            V(ts(T.thr[:, t + 1:t + 2], T.ai2[:], 11.0, None, A.add), ["ai2"], ["thr%d" % (t + 1)])
+        scan(4, 5)
+        cmp(4)
+        scan(5, 6)
+        cmp(5)
+        cnt(4, 6)
+        S(act(T.d0[:, 0::32], T.na15[:], AF.Copy), regs("na15", 0, 6), regs("d0", 0, 6))
+        dups(8, 12)
+        V(ts(T.indk[:], T.p3[:, 0:192], T.thr[:, t:t + 1], 1024.0, A.is_ge, A.mult), ["p3", th], ["indk"])
+        listmm("p7", 96, 12, "sel", "indk", 192)
+        P(mm(T.p6[:, 192:384], T.ctm[:], T.indk[:]), ["ctm", "indk"], ["p6"])
+        V(tt(T.eb[:, :, 0:16], T.eb[:, :, 0:16], T.mk[:], A.mult), ["mk"] + ["eb%d" % c for c in range(12)], ["eb"])
+
+        def lost(Q):
+            Q.matmul(T.p5[:, 0:192], T.cnb[:], T.tg[:, 192:384], True, False)
+            for c in range(12):
+                ins = Q.matmul(T.p5[:, 16 * c:192], T.cb[:], T.eb[:, c, 0:192 - 16 * c], False, c == 11)
+            return ins
+        P(lost, ["cnb", "cb", "tgg", "eb"] + ["eb%d" % c for c in range(12)], ["p5"])
+        V(tt(T.ya[:], T.tol[:], T.p7[:, 96:108], A.subtract), ["tol", "p7"], ["ya"])
+        V(tt(T.yb[:], T.p7[:, 96:108], T.mlf[:], A.min), ["p7", "mlf"], ["yb"])
+        V(tt(T.mn[:], T.ya[:], T.yb[:], A.max), ["ya", "yb"], ["mn"])
+        if not lastt:
+            V(cp(T["ms%d" % (t + 1)][:], T.mn[:]), ["mn"], ["ms%d" % (t + 1)])
+            send("mr%d" % (t + 1), "ms%d" % (t + 1), "ml%d" % (t + 1), 2 * t + 1)
+        else:
+            op("y", lambda Q: Q.dma_start(T.ym[:], T.mn[:]), ["mn"], ["ym"], ("outm", 16, True))
+        V(ts(T.oh[:], T.p6[:, 192:384], -1024.0, None, A.is_equal), ["p6"], ["oh"])
+        listmm("p6", 384, 12, "selk", "oh", 192, ("b32", "one12"))
+        dd = T.dd[:, 128 * t:128 * t + 128]
+        P(mm(T.p0[:, 0:192], dd, T.oh[:]), ["dda", "ddb", "oh"], ["p0"])
+        P(mm(T.p0[:, 192:384], dd, T.oh[:], True, False), ["dda", "ddb", "oh"], ["p0"])
+        P(mm(T.p0[:, 192:384], T.cb[:], T.c255[:], False, True), ["cb", "c255"], ["p0"])
+        use(4, 6)
+        V(ts(T.wn[:], T.p5[:, 0:192], -256.0, None, A.is_equal), ["p5"], ["wn"])
+        V(tt(T.si[:], T.wn[:], T.p6[:, 0:192], A.mult), ["wn", "p6"], ["si"])
+        listmm("p5", 448, 12, "sel", "si", 192, ("b512",))
+        V(cp(T.la[:], T.p6[:, 384:396]), ["p6"], ["la"])
+        V(tt(T.zdb[:], T[z][:], T.p0[:, 0:192], A.subtract), [z, "p0"], ["zdb"])
+        V(tt(T.yy[:], T.d0[:].indirect(T.la[:]), T.zdb[:], A.subtract), ["la", "zdb", "d0z"] + regs("d0", 0, 6), ["yy"])
+        V(tt(T.xx[:], T.yy[:], T.p0[:, 192:384], A.max), ["yy", "p0"], ["xx"])
+        if not lastt:
+            S(act(T["zs%d" % (t + 1)][:], T.xx[:], AF.Abs), ["xx"], ["zs%d" % (t + 1)])
+            send("zr%d" % (t + 1), "zs%d" % (t + 1), "zb%d" % (t + 1), 2 * t + 2)
+        else:
+            S(act(T.yzs[:], T.xx[:], AF.Abs), ["xx"], ["yzs"])
+            op("s", lambda Q: Q.dma_start(T.yz[:], T.yzs[:]), ["yzs"], ["yz"], ("outz", 16, True))
+        V(ts(T.p4[:, 192:384], T.p4[:, 0:192], 254.0, None, A.is_lt), ["p4"], ["p4", "ls"])
+        V(tt(T.fw[:], T.fd[:], T.p4[:, 192:384], A.mult), ["ls", "fd", "p4"], ["fw"])
+        V(ts(T.sl[:], T.p5[:, 448:460], 0.0625, None, A.mult), ["p5"], ["sl"])
+        V(tt(T.tb[:].indirect(T.sl[:]), T.fw[:], T.of[:], A.add), ["fw", "of", "sl"], ["tb"])
+
+    for t in range(STEPS):
+        step(t)
+
+    P(mm(T.p1[:, 0:256], T.cj[:], T.tb[:, 0:256]), ["cj", "tb"], ["p1"])
+    P(mm(T.p2[:, 0:256], T.cj[:], T.tb[:, 256:512]), ["cj", "tb"], ["p2"])
+    V(cp(T.yms[:, 0:256], T.p1[:, 0:256]), ["p1"], ["yma"])
+    S(act(T.yms[:, 256:512], T.p2[:, 0:256], AF.Copy), ["p2"], ["ymb"])
+    op("y", lambda Q: Q.dma_start(T.ymc[:, 0:256], T.yms[:, 0:256]), ["yma"], ["oa"], ("outa", 16, True))
+    op("s", lambda Q: Q.dma_start(T.ymc[:, 256:512], T.yms[:, 256:512]), ["ymb"], ["ob"], ("outb", 16, True))
+    emit()
+    for s in ("outm", "outz", "outa", "outb"):
+        g.wait_ge(T.sem[s], 16)
+    g.wait_ge(T.sem.snd, n_eng * 2 * (STEPS - 1))

@@ -15,7 +15,7 @@ for _names, _cols, _type in (
         ("mi", 12, I32), ("dvs", 5, B16), ("wts", 1, B16),
         ("d0 d1 ss", 6144, B16), ("ind", 3072, B16), ("ol", 192, U16), ("gg mb na15 r15 gi indk oh zdb xx wn", 192, B16),
         ("zt", 256, B16), ("tg", 384, F16), ("ui ua", 384, I32), ("tgs", 24, F32), ("mlf kl tol ya yb mn", 12, F32),
-        ("acc", 1, F32), ("ai ai2", 1, I32), ("thr", 8, F32), ("si", 192, F16), ("sl la", 12, U16),
+        ("acc", 1, F32), ("ai ai2", 1, I32), ("thr", 8, F32), ("si", 192, F16), ("sl la", 12, U16), ("es er", 24, F32), ("xs xr", 12, F32),
         ("yy yzs of fd fw", 192, F32), ("f1 f2 f3 f4", 192, I32),
         ("pi kki gri", 1, I32), ("pf kkf grf k37 kw jc jt", 1, F32), ("iw", 192, F32), ("ig cj onf", 128, F32), ("ie ce", 1536, B16),
         ("cid cidn c296 cb cbh tma tmb ctm cg4 cnb wb wb8", 128, B16), ("sel selk seln", 2048, B16), ("dg dd", 640, B16),
@@ -30,11 +30,12 @@ for _t in range(STEPS):
     if _t:
         SCRATCH["zs%d" % _t] = ("sbuf", [128, 192], B16)
         SCRATCH["ms%d" % _t] = ("sbuf", [128, 12], U16)
+del SCRATCH["ms1"]
 for _b in BANKS:
     SCRATCH[_b] = ("psum", [128, 512], F32)
 LOADS = ["mc", "m0", "z0", "ad", "gl", "pr", "wt", "dv"]
 SEMAPHORES = ["cv", "cs", "ct", "cg", "outz", "outm", "outa", "outb", "snd"] + ["ld_" + n for n in LOADS]
-SEMAPHORES += ["mr%d" % t for t in range(1, STEPS)] + ["zr%d" % t for t in range(1, STEPS)]
+SEMAPHORES += ["er"] + ["mr%d" % t for t in range(1, STEPS)] + ["zr%d" % t for t in range(1, STEPS)]
 
 
 def scheduler(g, T):
@@ -257,11 +258,19 @@ def rank_program(g, core, T, topo):
         lastt = t == STEPS - 1
         ml, z, th = "ml%d" % t, "zb%d" % t, "thr%d" % t
         if t:
-            op(None, None, [], [ml], ("mr%d" % t, n_eng, False))
+            op(None, None, [], [ml if t > 1 else "xr"], ("mr%d" % t, n_eng, False))
             op(None, None, [], [z], ("zr%d" % t, n_eng, False))
+        tol, mlf = (T.tol[:], T.mlf[:]) if t else (T.es[:, 0:12], T.es[:, 12:24])
+        if t == 1:
+            op(None, None, [], ["er"], ("er", n_eng, False))
+            V(tt(T.ya[:], T.er[:, 0:12], T.xr[:], A.subtract), ["er", "xr"], ["ya"])
+            V(tt(T.yb[:], T.xr[:], T.er[:, 12:24], A.min), ["er", "xr"], ["yb"])
+            V(tt(T.mn[:], T.ya[:], T.yb[:], A.max), ["ya", "yb"], ["mn"])
+            V(cp(T[ml][:], T.mn[:]), ["mn"], [ml])
 
         def na(a, b):
             S(act(T.d0[:, 1024 * a:1024 * b:2], T.adw[:].indirect(T.ol[:, 32 * a:32 * b]), AF.Copy, scale=-1.0), ["adw", "ol"], regs("d0", a, b))
+            S(act(T.na15[:, 32 * a:32 * b], T.d0[:, 1024 * a:1024 * b:32], AF.Copy), regs("d0", a, b), regs("na15", a, b))
 
         def pg(q, a, b):
             out, win = T.d1[:, 1024 * a + 1:1024 * b:2], T.prw[:].indirect(T.ol[:, 32 * a:32 * b])
@@ -270,13 +279,14 @@ def rank_program(g, core, T, topo):
         def scan(a, b):
             k = slice(1024 * a, 1024 * b, 32)
             c = slice(32 * a, 32 * b)
-            V(cp(T.na15[:, c], T.d0[:, k]), regs("d0", a, b), regs("na15", a, b))
             V(tt(T.d1[:, k], T.gg[:, c], T.d0[:, k], A.add), ["gg"] + regs("d0", a, b), regs("d1", a, b))
             V(ms(T.d0[:, k], -1024.0), [], regs("d0", a, b))
             j = slice(1024 * a, 1024 * b)
             V(lambda Q: Q.tensor_tensor_scan(T.ss[:, j], T.d0[:, j], T.d1[:, j], 0.0, A.add, A.max),
               ["d0z", "d1z"] + regs("d0", a, b) + regs("d1", a, b), regs("ss", a, b))
-            V(ts(T.r15[:, c], T.d1[:, k], 0.0, None, A.max), regs("d1", a, b), regs("r15", a, b))
+
+        def relu15(a, b):
+            V(ts(T.r15[:, 32 * a:32 * b], T.d1[:, 1024 * a:1024 * b:32], 0.0, None, A.max), regs("d1", a, b), regs("r15", a, b))
 
         def zexp(c):
             pb = "p%d" % (c % 2)
@@ -310,24 +320,23 @@ def rank_program(g, core, T, topo):
             for c in range(a, b):
                 V(ts(T.eb[:, c, 0:192 - 16 * c], T.tg[:, 16 * c:192], T.kl[:, c:c + 1], None, A.is_equal), ["tgt", "kl"], ["eb%d" % c])
 
-        def send(name, src, dst, k):
-            op("g", lambda Q: Q.remote_dma(T[dst][:], T[src][:], T.sem[name], T.sem.snd, pid, rid, mask_out), [src], [], ("snd", n_eng * k, False))
+        def send(name, src, dst, k, names=None):
+            op("g", lambda Q: Q.remote_dma(T[dst][:], T[src][:], T.sem[name], T.sem.snd, pid, rid, mask_out), names or [src], [], ("snd", n_eng * (k + 1), False))
 
+        S(act(T.gg[:], T.glw[:].indirect(T[ml][:]), AF.Copy), ["glw", ml], ["gg"])
+        S(act(T.mb[:], T.imw[:].indirect(T[ml][:]), AF.Copy), ["imwa", "imwb", ml], ["mb"])
         V(cp(T.ol[:], T.tb[:, 0:512].indirect(T[ml][:])), ["tb", ml], ["ol"])
         if t == 0:
             consts()
-        V(cp(T.mlf[:], T[ml][:]), [ml], ["mlf"])
-        na(0, 1)
+        V(cp(mlf, T[ml][:]), [ml], ["mlf"] + ["esm"] * (t == 0))
+        na(0, 2)
         pg("v", 0, 2)
         P(mm(T.p5[0:96, 0:128], T[z][:, 0:96], T.cid[:]), [z, "cid"], ["p5"])
         P(mm(T.p5[0:96, 128:256], T[z][:, 96:192], T.cid[:]), [z, "cid"], ["p5"])
-        S(act(T.gg[:], T.glw[:].indirect(T[ml][:]), AF.Copy), ["glw", ml], ["gg"])
-        na(1, 2)
         P(mm(T.p6[:, 0:192], T.cid[:], T[z][:], True, False), [z, "cid"], ["p6"])
         P(mm(T.p6[:, 0:192], T.cidn[:], T.gg[:], False, True), ["cidn", "gg"], ["p6"])
         S(act(T.zt[0:96, :], T.p5[0:96, 0:256], AF.Copy), ["p5"], ["zt"])
         S(act(T.gi[:], T.p6[:, 0:192], AF.Sign, bias=0.5), ["p6"], ["gi"])
-        S(act(T.mb[:], T.imw[:].indirect(T[ml][:]), AF.Copy), ["imwa", "imwb", ml], ["mb"])
         na(2, 4)
         S(act(T.of[:], T.tb[:, 0:512].indirect(T[ml][:]), AF.Copy), ["tb", ml], ["of"])
         zexp(0)
@@ -336,8 +345,7 @@ def rank_program(g, core, T, topo):
         P(mm(T.p6[:, 0:192], T.wb[:], T[z][:]), ["wb", z], ["p6"])
         P(mm(T.p6[:, 192:384], T.wb8[:], T[z][:], True, False), ["wb8", z], ["p6"])
         P(mm(T.p6[:, 192:384], T.c296[:], T.mb[:], False, True), ["c296", "mb"], ["p6"])
-        scan(0, 1)
-        scan(1, 2)
+        scan(0, 2)
         V(ts(T.tg[:, 192:384], T.p5[:, 256:448], 8.0, T.thr[:, t:t + 1], A.add, A.is_ge), ["p5", th], ["tgg"])
         V(cp(T.ui[:], T.p6[:, 0:384]), ["p6"], ["ui"])
         V(ts(T.ua[:], T.ui[:], 4095, None, A.bitwise_and), ["ui"], ["ua"])
@@ -347,14 +355,17 @@ def rank_program(g, core, T, topo):
         cmp(0)
         cmp(1)
         listmm("p7", 0, 24, "sel", "tg", 384, (), ["tgg", "tgt"])
-        S(act(T.tgs[:, 0:12], T.p7[:, 0:12], AF.Copy, scale=0.0625), ["p7"], ["tgsa"])
-        S(act(T.tgs[:, 12:24], T.p7[:, 12:24], AF.Copy, scale=0.0625, accum_out=T.acc[:]), ["p7"], ["tgsb", "acc"])
-        S(act(T.tol[:], T.p7[:, 0:12], AF.Copy, scale=0.0625, bias=-1.0), ["p7"], ["tol"])
-        if not lastt:
-            P(mm(T.p7[:, 64:65], T.onf[:], T.acc[:]), ["onf", "acc"], ["p7"])
         S(act(T.p2[:, 0:192], T.of[:], AF.Copy), ["of"], ["p2"])
         S(act(T.p2[:, 192:384], T.of[:], AF.Identity, bias=T.k37[:]), ["of", "k37"], ["p2"])
-        pg("s", 2, 4)
+        pg("s", 2, 3)
+        S(act(T.tgs[:, 0:12], T.p7[:, 0:12], AF.Copy, scale=0.0625), ["p7"], ["tgsa"])
+        S(act(T.tgs[:, 12:24], T.p7[:, 12:24], AF.Copy, scale=0.0625, accum_out=T.acc[:]), ["p7"], ["tgsb", "acc"])
+        S(act(tol, T.p7[:, 0:12], AF.Copy, scale=0.0625, bias=-1.0), ["p7"], ["tol"] + ["est"] * (t == 0))
+        if t == 0:
+            send("er", "es", "er", 0, ["est", "esm"])
+        if not lastt:
+            P(mm(T.p7[:, 64:65], T.onf[:], T.acc[:]), ["onf", "acc"], ["p7"])
+        pg("s", 3, 4)
         zexp(2)
         zexp(3)
         cnt(0, 2)
@@ -362,6 +373,7 @@ def rank_program(g, core, T, topo):
         V(ts(T.f2[:], T.f1[:], 5, None, A.arith_shift_right), ["f1"], ["f2"])
         V(tt(T.kl[:], T.tgs[:, 0:12], T.tgs[:, 12:24], A.mult), ["tgsa", "tgsb"], ["kl"])
         dups(0, 8)
+        relu15(0, 2)
         use(0, 2)
         na(4, 6)
         pg("s", 4, 5)
@@ -374,9 +386,7 @@ def rank_program(g, core, T, topo):
         P(mm(T.p6[:, 0:192], T.cid[:], T.tg[:, 0:192], True, False), ["cid", "tgt"], ["p6"])
         P(mm(T.p6[:, 0:192], T.cid[:], T.ns[:], False, True), ["cid", "ns"], ["p6"])
         cnt(2, 4)
-        V(tt(T.f3[:], T.f2[:], T.p2[:, 192:384], A.add), ["f2", "p2"], ["f3"])
-        V(ts(T.f4[:], T.f3[:], 4095, None, A.bitwise_and), ["f3"], ["f4"])
-        V(tt(T.fd[:], T.f4[:], T.p2[:, 0:192], A.subtract), ["f4", "p2"], ["fd"])
+        relu15(2, 4)
         use(2, 4)
         if not lastt:
             V(cp(T.ai[:], T.p7[:, 64:65]), ["p7"], ["ai"])
@@ -386,6 +396,7 @@ def rank_program(g, core, T, topo):
         cmp(4)
         scan(5, 6)
         cmp(5)
+        relu15(4, 6)
         cnt(4, 6)
         S(act(T.d0[:, 0::32], T.na15[:], AF.Copy), regs("na15", 0, 6), regs("d0", 0, 6))
         dups(8, 12)
@@ -400,22 +411,29 @@ def rank_program(g, core, T, topo):
                 ins = Q.matmul(T.p5[:, 16 * c:192], T.cb[:], T.eb[:, c, 0:192 - 16 * c], False, c == 11)
             return ins
         P(lost, ["cnb", "cb", "tgg", "eb"] + ["eb%d" % c for c in range(12)], ["p5"])
-        V(tt(T.ya[:], T.tol[:], T.p7[:, 96:108], A.subtract), ["tol", "p7"], ["ya"])
-        V(tt(T.yb[:], T.p7[:, 96:108], T.mlf[:], A.min), ["p7", "mlf"], ["yb"])
-        V(tt(T.mn[:], T.ya[:], T.yb[:], A.max), ["ya", "yb"], ["mn"])
-        if not lastt:
+        if t:
+            V(tt(T.ya[:], tol, T.p7[:, 96:108], A.subtract), ["tol", "p7"], ["ya"])
+            V(tt(T.yb[:], T.p7[:, 96:108], mlf, A.min), ["p7", "mlf"], ["yb"])
+            V(tt(T.mn[:], T.ya[:], T.yb[:], A.max), ["ya", "yb"], ["mn"])
+        if t == 0:
+            V(cp(T.xs[:], T.p7[:, 96:108]), ["p7"], ["xs"])
+            send("mr1", "xs", "xr", 1)
+        elif not lastt:
             V(cp(T["ms%d" % (t + 1)][:], T.mn[:]), ["mn"], ["ms%d" % (t + 1)])
             send("mr%d" % (t + 1), "ms%d" % (t + 1), "ml%d" % (t + 1), 2 * t + 1)
         else:
             op("y", lambda Q: Q.dma_start(T.ym[:], T.mn[:]), ["mn"], ["ym"], ("outm", 16, True))
-        V(ts(T.oh[:], T.p6[:, 192:384], -1024.0, None, A.is_equal), ["p6"], ["oh"])
+        S(act(T.oh[:], T.p6[:, 192:384], AF.Relu, scale=-0.0009765625), ["p6"], ["oh"])
         listmm("p6", 384, 12, "selk", "oh", 192, ("b32", "one12"))
         dd = T.dd[:, 128 * t:128 * t + 128]
         P(mm(T.p0[:, 0:192], dd, T.oh[:]), ["dda", "ddb", "oh"], ["p0"])
         P(mm(T.p0[:, 192:384], dd, T.oh[:], True, False), ["dda", "ddb", "oh"], ["p0"])
         P(mm(T.p0[:, 192:384], T.cb[:], T.c255[:], False, True), ["cb", "c255"], ["p0"])
         use(4, 6)
-        V(ts(T.wn[:], T.p5[:, 0:192], -256.0, None, A.is_equal), ["p5"], ["wn"])
+        S(act(T.wn[:], T.p5[:, 0:192], AF.Relu, bias=-255.0, scale=-1.0), ["p5"], ["wn"])
+        V(tt(T.f3[:], T.f2[:], T.p2[:, 192:384], A.add), ["f2", "p2"], ["f3"])
+        V(ts(T.f4[:], T.f3[:], 4095, None, A.bitwise_and), ["f3"], ["f4"])
+        V(tt(T.fd[:], T.f4[:], T.p2[:, 0:192], A.subtract), ["f4", "p2"], ["fd"])
         V(tt(T.si[:], T.wn[:], T.p6[:, 0:192], A.mult), ["wn", "p6"], ["si"])
         listmm("p5", 448, 12, "sel", "si", 192, ("b512",))
         V(cp(T.la[:], T.p6[:, 384:396]), ["p6"], ["la"])
@@ -445,4 +463,4 @@ def rank_program(g, core, T, topo):
     emit()
     for s in ("outm", "outz", "outa", "outb"):
         g.wait_ge(T.sem[s], 16)
-    g.wait_ge(T.sem.snd, n_eng * 2 * (STEPS - 1))
+    g.wait_ge(T.sem.snd, n_eng * (2 * (STEPS - 1) + 1))

from concourse.mybir import dt, AluOpType, AxisListType, ActivationFunctionType

A = AluOpType
AF = ActivationFunctionType
STEPS = 5
B16 = "bfloat16"
F32 = "float32"
F16 = "float16"
I32 = "int32"
U16 = "uint16"
BANKS = ["p%d" % b for b in range(8)]
SCRATCH = {}
for _names, _cols, _type in (
        ("prw adw", 4096, B16), ("glw imw", 512, B16), ("mci", 512, I32), ("mcf yms", 512, F32), ("tb", 704, F32),
        ("mi", 12, I32), ("dvs", 5, B16), ("wts", 1, B16),
        ("d0 d1 ss", 6144, B16), ("ind", 3072, B16), ("ol", 192, U16), ("gg mb na15 r15 gi indk oh zdb xx wn", 192, B16),
        ("zt", 256, B16), ("tg", 384, F16), ("ui ua", 384, I32), ("tgs", 24, F32), ("mlf kl tol ya yb mn", 12, F32),
        ("acc", 1, F32), ("ai ai2", 1, I32), ("thr", 8, F32), ("si", 192, F16), ("sl la", 12, U16), ("es er", 24, F32), ("xs xr", 12, F32),
        ("yy yzs of fd fw", 192, F32), ("f1 f2 f3 f4", 192, I32),
        ("pi kki gri", 1, I32), ("pf kkf grf k37 kw jc jt", 1, F32), ("iw", 192, F32), ("ig cj onf", 128, F32), ("ie ce", 1536, B16),
        ("cid cidn c296 cb cbh tma tmb ctm cg4 cnb wb wb8", 128, B16), ("sel selk seln", 2048, B16), ("dg dd", 640, B16),
        ("ic bl", 12, F32), ("b32 one12", 12, B16), ("b512", 12, F16), ("ns", 192, F16), ("c255", 192, B16)):
    for _n in _names.split():
        SCRATCH[_n] = ("sbuf", [128, _cols], _type)
SCRATCH["eb"] = ("sbuf", [128, 12, 208], B16)
SCRATCH["mk"] = ("sbuf", [128, 12, 16], B16)
for _t in range(STEPS):
    SCRATCH["zb%d" % _t] = ("sbuf", [128, 192], B16)
    SCRATCH["ml%d" % _t] = ("sbuf", [128, 12], U16)
    if _t:
        SCRATCH["zs%d" % _t] = ("sbuf", [128, 192], B16)
        SCRATCH["ms%d" % _t] = ("sbuf", [128, 12], U16)
del SCRATCH["ms1"]
for _b in BANKS:
    SCRATCH[_b] = ("psum", [128, 512], F32)
LOADS = ["mc", "m0", "z0", "ad", "gl", "pr", "wt", "dv"]
SEMAPHORES = ["cv", "cs", "ct", "cg", "outz", "outm", "outa", "outb", "snd"] + ["ld_" + n for n in LOADS]
SEMAPHORES += ["er"] + ["mr%d" % t for t in range(1, STEPS)] + ["zr%d" % t for t in range(1, STEPS)]


def scheduler(g, T):
    queues = {"g": g, "v": g.vector, "s": g.scalar, "t": g.tensor, "y": g.sync}
    ops = []
    wr, rd, bank = {}, {}, {}

    def op(q, fn, r=(), w=(), ext=None):
        i = len(ops)
        deps = set()
        for x in list(r) + list(w):
            if x in BANKS:
                h = bank.setdefault(x, {})
                deps.update(h[k] for k in h if k != q or (q != "t" and x in w))
                h[q] = i
        for x in r:
            if x not in BANKS:
                if x in wr:
                    deps.add(wr[x])
                rd.setdefault(x, {})[q] = i
        for x in w:
            if x not in BANKS:
                if x in wr:
                    deps.add(wr[x])
                deps.update(rd.get(x, {}).values())
                wr[x] = i
                rd[x] = {}
        deps.discard(i)
        ops.append({"q": q, "fn": fn, "deps": deps, "ext": ext})

    def emit():
        pos, known, snap, need, waits = {}, {}, [], set(), []
        for i, o in enumerate(ops):
            q = o["q"]
            pos[q] = pos.get(q, 0) + 1
            o["pos"] = pos[q]
            k = known.setdefault(q, {})
            mine = []
            for d in sorted(o["deps"], reverse=True):
                e = ops[d]["ext"]
                key, val = (e[0], e[1]) if e else (ops[d]["q"], ops[d]["pos"])
                if k.get(key, 0) >= val:
                    continue
                mine.append(d)
                need.add(d)
                for a, b in snap[d].items():
                    k[a] = max(k.get(a, 0), b)
                k[key] = max(k.get(key, 0), val)
            waits.append(mine)
            snap.append(dict(k))
        last = {}
        for i, o in enumerate(ops):
            if not o["ext"]:
                last[o["q"]] = i
        need.update(last.values())
        count = {}
        for i, o in enumerate(ops):
            if i in need and not o["ext"]:
                count[o["q"]] = count.get(o["q"], 0) + 1
                o["tok"] = ("c" + o["q"], count[o["q"]])
        for i, o in enumerate(ops):
            if o["fn"] is None:
                continue
            Q = queues[o["q"]]
            best = {}
            for d in waits[i]:
                s, n = (ops[d]["ext"] or ops[d]["tok"])[:2]
                best[s] = max(best.get(s, 0), n)
            for s, n in best.items():
                Q.wait_ge(T.sem[s], n)
            ins = o["fn"](Q)
            if o["ext"]:
                if o["ext"][2]:
                    ins.then_inc(T.sem[o["ext"][0]], 16)
            elif i in need:
                ins.then_inc(T.sem["c" + o["q"]], 1)
        for q, n in count.items():
            g.wait_ge(T.sem["c" + q], n)

    return op, emit


def regs(name, a, b):
    return ["%s.%d" % (name, c) for c in range(a, b)]


def rank_program(g, core, T, topo):
    rank = T.rank_of(core)
    if rank is None:
        return
    op, emit = scheduler(g, T)
    n_ranks = len(T.cores)
    nxt = T.cores[(rank + 1) % n_ranks]
    n_eng = 8
    mask_out = sum(1 << e for e in topo.engines(core, nxt)[:n_eng])
    rid, pid = topo.addr(nxt)[:2]

    def V(fn, r=(), w=()):
        op("v", fn, r, w)

    def S(fn, r=(), w=()):
        op("s", fn, r, w)

    def P(fn, r=(), w=()):
        op("t", fn, r, w)

    def G(fn, r=(), w=()):
        op("g", fn, r, w)

    def ts(out, in0, s1, s2, *o):
        return lambda Q: Q.tensor_scalar(out, in0, s1, s2, *o)

    def tt(out, a, b, o):
        return lambda Q: Q.tensor_tensor(out, a, b, o)

    def cp(out, a):
        return lambda Q: Q.tensor_copy(out, a)

    def act(out, a, f, **k):
        return lambda Q: Q.activation(out, a, f, **k)

    def ms(out, c):
        return lambda Q: Q.memset(out, c)

    def mm(out, a, b, start=True, stop=True):
        return lambda Q: Q.matmul(out, a, b, start, stop)

    def iota(out, pattern, base=0, cm=0):
        return lambda Q: Q.iota(out, pattern, base, cm, allow_small_or_imprecise_dtypes=True)

    def load(q, name, buf):
        op(q, lambda Q: Q.dma_start(T[buf][:], T[name][:]), [], [buf], ("ld_" + name, 16, True))

    load("y", "mc", "mci")
    load("s", "m0", "mi")
    load("y", "ad", "adw")
    load("s", "pr", "prw")
    load("y", "gl", "glw")
    load("y", "z0", "zb0")
    load("y", "wt", "wts")
    load("y", "dv", "dvs")

    G(lambda Q: Q.iota(T.pi[:], [[0, 1]], 0, 1), [], ["pi"])
    G(iota(T.ig[:], [[1, 8], [0, 16]]), [], ["ig"])
    G(iota(T.iw[:], [[1, 192]]), [], ["iw"])
    G(iota(T.ie[:], [[1, 96], [0, 16]]), [], ["ie"])
    G(iota(T.ic[:], [[16, 12]]), [], ["ic"])
    G(iota(T.imw[:, 0:256], [[1, 256]]), [], ["imwa"])
    G(iota(T.imw[:, 256:512], [[1, 256]], -256), [], ["imwb"])
    V(ms(T.d0[:, 1::2], 0.0), [], ["d0z"])
    V(ms(T.sel[:], 0.0), [], ["selz"])
    V(ts(T.kki[:], T.pi[:], 15, None, A.bitwise_and), ["pi"], ["kki"])
    V(ts(T.gri[:], T.pi[:], 4, None, A.arith_shift_right), ["pi"], ["gri"])
    V(cp(T.pf[:], T.pi[:]), ["pi"], ["pf"])
    V(cp(T.kkf[:], T.kki[:]), ["kki"], ["kkf"])
    V(cp(T.grf[:], T.gri[:]), ["gri"], ["grf"])
    V(ts(T.kw[:], T.kkf[:], 2.0, -1.0, A.mult, A.add), ["kkf"], ["kw"])
    V(ts(T.cb[:], T.ig[:], T.grf[:], None, A.is_equal), ["ig", "grf"], ["cb"])
    for i in range(16):
        V(cp(T.sel[:, 129 * i:129 * i + 113:16], T.cb[:, 0::16]), ["cb", "selz"], ["sel"] if i == 15 else [])
    S(act(T.d1[:, 0::2], T.d0[:, 1::2], AF.Copy), ["d0z"], ["d1z"])
    S(act(T.seln[:], T.sel[:], AF.Copy, scale=-1.0), ["sel"], ["seln"])
    S(act(T.selk[:], T.sel[:], AF.Copy, scale=T.kw[:]), ["sel", "kw"], ["selk"])
    V(ts(T.k37[:], T.kkf[:], -37.0, 555.0, A.mult, A.add), ["kkf"], ["k37"])
    V(tt(T.jt[:], T.pf[:], T.kw[:], A.subtract), ["pf", "kw"], ["jt"])
    V(ts(T.jc[:], T.jt[:], 14.0, None, A.add), ["jt"], ["jc"])
    V(ts(T.cj[:], T.iw[:, 0:128], T.jc[:], None, A.is_equal), ["iw", "jc"], ["cj"])
    V(cp(T.mcf[:], T.mci[:]), ["mci"], ["mcf"])
    P(mm(T.p0[:], T.cj[:], T.mcf[:]), ["cj", "mcf"], ["p0"])
    V(cp(T.ml0[:], T.mi[:]), ["mi"], ["ml0"])
    V(ts(T.cid[:], T.iw[:, 0:128], T.pf[:], None, A.is_equal), ["iw", "pf"], ["cid"])
    V(cp(T.tb[:, 0:512], T.p0[:]), ["p0"], ["tb"])

    def consts():
        V(ts(T.ce[:], T.ie[:], T.pf[:], None, A.is_equal), ["ie", "pf"], ["ce"])
        V(ts(T.cidn[:], T.cid[:], -1.0, None, A.mult), ["cid"], ["cidn"])
        V(ts(T.c296[:], T.cid[:], 296.0, None, A.mult), ["cid"], ["c296"])
        V(ts(T.cg4[:], T.cb[:], -4.0, None, A.mult), ["cb"], ["cg4"])
        V(ts(T.cbh[:], T.cb[:], 0.5, None, A.mult), ["cb"], ["cbh"])
        V(ts(T.cnb[:], T.cb[:], -16.0, None, A.mult), ["cb"], ["cnb"])
        V(ms(T.thr[:], 11.0), [], ["thr0"])
        for c in range(12):
            V(ts(T.mk[:, c, :], T.iw[:, 0:16], T.kkf[:], None, A.is_gt), ["iw", "kkf"], ["mk"] if c == 11 else [])
        V(ts(T.tma[:], T.iw[:, 0:128], T.pf[:], 2.0, A.is_gt, A.mult), ["iw", "pf"], ["tma"])
        V(tt(T.tmb[:], T.tma[:], T.cb[:], A.mult), ["tma", "cb"], ["tmb"])
        V(tt(T.ctm[:], T.tmb[:], T.cid[:], A.subtract), ["tmb", "cid"], ["ctm"])
        V(ts(T.bl[:], T.ic[:], T.kkf[:], None, A.add), ["ic", "kkf"], ["bl"])
        V(ts(T.b32[:], T.bl[:], 32.0, None, A.mult), ["bl"], ["b32"])
        V(ts(T.b512[:], T.bl[:], 512.0, 16.0, A.add, A.mult), ["bl"], ["b512"])
        V(ms(T.one12[:], 1.0), [], ["one12"])
        V(ts(T.ns[:], T.iw[:], -1.0, -513.0, A.mult, A.add), ["iw"], ["ns"])
        V(ms(T.c255[:], -15.9375), [], ["c255"])
        V(ms(T.onf[:], 1.0), [], ["onf"])
        V(ts(T.wb[:], T.cb[:], T.wts[:], None, A.mult), ["cb", "wts"], ["wb"])
        V(ts(T.wb8[:], T.cb[:], T.wts[:], 8.0, A.mult, A.mult), ["cb", "wts"], ["wb8"])
        for t in range(STEPS):
            V(ts(T.dg[:, 128 * t:128 * t + 128], T.cid[:], T.dvs[:, t:t + 1], None, A.mult), ["cid", "dvs"], ["dg%d" % t])

    def distances():
        for t in range(STEPS):
            P(mm(T.p2[:, 128 * (t % 4):128 * (t % 4) + 128], T.cb[:], T.dg[:, 128 * t:128 * t + 128]), ["cb", "dg%d" % t], ["p2"])
            if t == 3:
                S(act(T.dd[:, 0:512], T.p2[:], AF.Copy), ["p2"], ["dda"])
        S(act(T.dd[:, 512:640], T.p2[:, 0:128], AF.Copy), ["p2"], ["ddb"])

    def listmm(pb, col, width, mats, buf, total, base=(), names=None):
        def fn(Q):
            out = T[pb][:, col:col + width]
            first = True
            for b in base:
                Q.matmul(out, T.cid[:], T[b][:], first, False)
                first = False
            for i in range(16):
                ins = Q.matmul(out, T[mats][:, 128 * i:128 * i + 128], T[buf][:, i:total:16], first, i == 15)
                first = False
            return ins
        P(fn, ["cid", mats] + (names or [buf]) + list(base), [pb])

    def step(t):
        lastt = t == STEPS - 1
        ml, z, th = "ml%d" % t, "zb%d" % t, "thr%d" % t
        if t:
            op(None, None, [], [ml if t > 1 else "xr"], ("mr%d" % t, n_eng, False))
            op(None, None, [], [z], ("zr%d" % t, n_eng, False))
        tol, mlf = (T.tol[:], T.mlf[:]) if t else (T.es[:, 0:12], T.es[:, 12:24])
        if t == 1:
            op(None, None, [], ["er"], ("er", n_eng, False))
            V(tt(T.ya[:], T.er[:, 0:12], T.xr[:], A.subtract), ["er", "xr"], ["ya"])
            V(tt(T.yb[:], T.xr[:], T.er[:, 12:24], A.min), ["er", "xr"], ["yb"])
            V(tt(T.mn[:], T.ya[:], T.yb[:], A.max), ["ya", "yb"], ["mn"])
            V(cp(T[ml][:], T.mn[:]), ["mn"], [ml])

        def na(a, b):
            S(act(T.d0[:, 1024 * a:1024 * b:2], T.adw[:].indirect(T.ol[:, 32 * a:32 * b]), AF.Copy, scale=-1.0), ["adw", "ol"], regs("d0", a, b))
            S(act(T.na15[:, 32 * a:32 * b], T.d0[:, 1024 * a:1024 * b:32], AF.Copy), regs("d0", a, b), regs("na15", a, b))

        def pg(q, a, b):
            out, win = T.d1[:, 1024 * a + 1:1024 * b:2], T.prw[:].indirect(T.ol[:, 32 * a:32 * b])
            op(q, cp(out, win) if q == "v" else act(out, win, AF.Copy), ["prw", "ol"], regs("d1", a, b))

        def scan(a, b):
            k = slice(1024 * a, 1024 * b, 32)
            c = slice(32 * a, 32 * b)
            V(tt(T.d1[:, k], T.gg[:, c], T.d0[:, k], A.add), ["gg"] + regs("d0", a, b), regs("d1", a, b))
            V(ms(T.d0[:, k], -1024.0), [], regs("d0", a, b))
            j = slice(1024 * a, 1024 * b)
            V(lambda Q: Q.tensor_tensor_scan(T.ss[:, j], T.d0[:, j], T.d1[:, j], 0.0, A.add, A.max),
              ["d0z", "d1z"] + regs("d0", a, b) + regs("d1", a, b), regs("ss", a, b))

        def relu15(a, b):
            V(ts(T.r15[:, 32 * a:32 * b], T.d1[:, 1024 * a:1024 * b:32], 0.0, None, A.max), regs("d1", a, b), regs("r15", a, b))

        def zexp(c):
            pb = "p%d" % (c % 2)
            P(mm(T[pb][:], T.zt[0:96, 128 * (c // 3):128 * (c // 3) + 128], T.ce[0:96, 512 * (c % 3):512 * (c % 3) + 512]), ["zt", "ce"], [pb])

        def cmp(c):
            pb = "p%d" % (c % 2)
            V(tt(T.ind[:, 512 * c:512 * c + 512], T.ss[:, 1024 * c + 1:1024 * c + 1024:2], T[pb][:], A.is_le), regs("ss", c, c + 1) + [pb], regs("ind", c, c + 1))

        def cnt(a, b):
            def fn(Q):
                out = T.p3[:, 32 * a:32 * b]
                Q.matmul(out, T.cg4[:], T.tg[:, 192 + 32 * a:192 + 32 * b], True, False)
                for k in range(16):
                    ins = Q.matmul(out, T.sel[:, 128 * k:128 * k + 128], T.ind[:, 512 * a + k:512 * b:16], False, k == 15)
                return ins
            P(fn, ["sel", "cg4", "tgg"] + regs("ind", a, b), ["p3"])

        def use(a, b):
            def fn(Q):
                out = T.p4[:, 32 * a:32 * b]
                Q.matmul(out, T.sel[:, 0:128], T.gg[:, 32 * a:32 * b], True, False)
                Q.matmul(out, T.seln[:, 0:128], T.r15[:, 32 * a:32 * b], False, False)
                for k in range(1, 16):
                    Q.matmul(out, T.sel[:, 128 * k:128 * k + 128], T.ss[:, 1024 * a + 2 * k - 1:1024 * b:32], False, False)
                    ins = Q.matmul(out, T.seln[:, 128 * k:128 * k + 128], T.ss[:, 1024 * a + 2 * k:1024 * b:32], False, k == 15)
                return ins
            P(fn, ["sel", "seln", "gg"] + regs("r15", a, b) + regs("ss", a, b), ["p4"])

        def dups(a, b):
            for c in range(a, b):
                V(ts(T.eb[:, c, 0:192 - 16 * c], T.tg[:, 16 * c:192], T.kl[:, c:c + 1], None, A.is_equal), ["tgt", "kl"], ["eb%d" % c])

        def send(name, src, dst, k, names=None):
            op("g", lambda Q: Q.remote_dma(T[dst][:], T[src][:], T.sem[name], T.sem.snd, pid, rid, mask_out), names or [src], [], ("snd", n_eng * (k + 1), False))

        S(act(T.gg[:], T.glw[:].indirect(T[ml][:]), AF.Copy), ["glw", ml], ["gg"])
        S(act(T.mb[:], T.imw[:].indirect(T[ml][:]), AF.Copy), ["imwa", "imwb", ml], ["mb"])
        V(cp(T.ol[:], T.tb[:, 0:512].indirect(T[ml][:])), ["tb", ml], ["ol"])
        if t == 0:
            consts()
        V(cp(mlf, T[ml][:]), [ml], ["mlf"] + ["esm"] * (t == 0))
        na(0, 2)
        pg("v", 0, 2)
        P(mm(T.p5[0:96, 0:128], T[z][:, 0:96], T.cid[:]), [z, "cid"], ["p5"])
        P(mm(T.p5[0:96, 128:256], T[z][:, 96:192], T.cid[:]), [z, "cid"], ["p5"])
        P(mm(T.p6[:, 0:192], T.cid[:], T[z][:], True, False), [z, "cid"], ["p6"])
        P(mm(T.p6[:, 0:192], T.cidn[:], T.gg[:], False, True), ["cidn", "gg"], ["p6"])
        S(act(T.zt[0:96, :], T.p5[0:96, 0:256], AF.Copy), ["p5"], ["zt"])
        S(act(T.gi[:], T.p6[:, 0:192], AF.Sign, bias=0.5), ["p6"], ["gi"])
        na(2, 4)
        S(act(T.of[:], T.tb[:, 0:512].indirect(T[ml][:]), AF.Copy), ["tb", ml], ["of"])
        zexp(0)
        zexp(1)
        P(mm(T.p5[:, 256:448], T.cbh[:], T.gi[:]), ["cbh", "gi"], ["p5"])
        P(mm(T.p6[:, 0:192], T.wb[:], T[z][:]), ["wb", z], ["p6"])
        P(mm(T.p6[:, 192:384], T.wb8[:], T[z][:], True, False), ["wb8", z], ["p6"])
        P(mm(T.p6[:, 192:384], T.c296[:], T.mb[:], False, True), ["c296", "mb"], ["p6"])
        scan(0, 2)
        V(ts(T.tg[:, 192:384], T.p5[:, 256:448], 8.0, T.thr[:, t:t + 1], A.add, A.is_ge), ["p5", th], ["tgg"])
        V(cp(T.ui[:], T.p6[:, 0:384]), ["p6"], ["ui"])
        V(ts(T.ua[:], T.ui[:], 4095, None, A.bitwise_and), ["ui"], ["ua"])
        V(ts(T.tg[:, 0:192], T.ua[:, 192:384], 0.125, 1.0, A.mult, A.add), ["ua"], ["tgt"])
        if t == 0:
            distances()
        cmp(0)
        cmp(1)
        listmm("p7", 0, 24, "sel", "tg", 384, (), ["tgg", "tgt"])
        S(act(T.p2[:, 0:192], T.of[:], AF.Copy), ["of"], ["p2"])
        S(act(T.p2[:, 192:384], T.of[:], AF.Identity, bias=T.k37[:]), ["of", "k37"], ["p2"])
        pg("s", 2, 3)
        S(act(T.tgs[:, 0:12], T.p7[:, 0:12], AF.Copy, scale=0.0625), ["p7"], ["tgsa"])
        S(act(T.tgs[:, 12:24], T.p7[:, 12:24], AF.Copy, scale=0.0625, accum_out=T.acc[:]), ["p7"], ["tgsb", "acc"])
        S(act(tol, T.p7[:, 0:12], AF.Copy, scale=0.0625, bias=-1.0), ["p7"], ["tol"] + ["est"] * (t == 0))
        if t == 0:
            send("er", "es", "er", 0, ["est", "esm"])
        if not lastt:
            P(mm(T.p7[:, 64:65], T.onf[:], T.acc[:]), ["onf", "acc"], ["p7"])
        pg("s", 3, 4)
        zexp(2)
        zexp(3)
        cnt(0, 2)
        V(tt(T.f1[:], T.ua[:, 0:192], T.p2[:, 0:192], A.mult), ["p2", "ua"], ["f1"])
        V(ts(T.f2[:], T.f1[:], 5, None, A.arith_shift_right), ["f1"], ["f2"])
        V(tt(T.kl[:], T.tgs[:, 0:12], T.tgs[:, 12:24], A.mult), ["tgsa", "tgsb"], ["kl"])
        dups(0, 8)
        relu15(0, 2)
        use(0, 2)
        na(4, 6)
        pg("s", 4, 5)
        pg("s", 5, 6)
        scan(2, 4)
        cmp(2)
        cmp(3)
        zexp(4)
        zexp(5)
        P(mm(T.p6[:, 0:192], T.cid[:], T.tg[:, 0:192], True, False), ["cid", "tgt"], ["p6"])
        P(mm(T.p6[:, 0:192], T.cid[:], T.ns[:], False, True), ["cid", "ns"], ["p6"])
        cnt(2, 4)
        relu15(2, 4)
        use(2, 4)
        if not lastt:
            V(cp(T.ai[:], T.p7[:, 64:65]), ["p7"], ["ai"])
            V(ts(T.ai2[:], T.ai[:], 1, None, A.bitwise_and), ["ai"], ["ai2"])
            V(ts(T.thr[:, t + 1:t + 2], T.ai2[:], 11.0, None, A.add), ["ai2"], ["thr%d" % (t + 1)])
        scan(4, 5)
        cmp(4)
        scan(5, 6)
        cmp(5)
        relu15(4, 6)
        cnt(4, 6)
        S(act(T.d0[:, 0::32], T.na15[:], AF.Copy), regs("na15", 0, 6), regs("d0", 0, 6))
        dups(8, 12)
        V(ts(T.indk[:], T.p3[:, 0:192], T.thr[:, t:t + 1], 1024.0, A.is_ge, A.mult), ["p3", th], ["indk"])
        listmm("p7", 96, 12, "sel", "indk", 192)
        P(mm(T.p6[:, 192:384], T.ctm[:], T.indk[:]), ["ctm", "indk"], ["p6"])
        V(tt(T.eb[:, :, 0:16], T.eb[:, :, 0:16], T.mk[:], A.mult), ["mk"] + ["eb%d" % c for c in range(12)], ["eb"])

        def lost(Q):
            Q.matmul(T.p5[:, 0:192], T.cnb[:], T.tg[:, 192:384], True, False)
            for c in range(12):
                ins = Q.matmul(T.p5[:, 16 * c:192], T.cb[:], T.eb[:, c, 0:192 - 16 * c], False, c == 11)
            return ins
        P(lost, ["cnb", "cb", "tgg", "eb"] + ["eb%d" % c for c in range(12)], ["p5"])
        if t:
            V(tt(T.ya[:], tol, T.p7[:, 96:108], A.subtract), ["tol", "p7"], ["ya"])
            V(tt(T.yb[:], T.p7[:, 96:108], mlf, A.min), ["p7", "mlf"], ["yb"])
            V(tt(T.mn[:], T.ya[:], T.yb[:], A.max), ["ya", "yb"], ["mn"])
        if t == 0:
            V(cp(T.xs[:], T.p7[:, 96:108]), ["p7"], ["xs"])
            send("mr1", "xs", "xr", 1)
        elif not lastt:
            V(cp(T["ms%d" % (t + 1)][:], T.mn[:]), ["mn"], ["ms%d" % (t + 1)])
            send("mr%d" % (t + 1), "ms%d" % (t + 1), "ml%d" % (t + 1), 2 * t + 1)
        else:
            op("y", lambda Q: Q.dma_start(T.ym[:], T.mn[:]), ["mn"], ["ym"], ("outm", 16, True))
        S(act(T.oh[:], T.p6[:, 192:384], AF.Relu, scale=-0.0009765625), ["p6"], ["oh"])
        listmm("p6", 384, 12, "selk", "oh", 192, ("b32", "one12"))
        dd = T.dd[:, 128 * t:128 * t + 128]
        P(mm(T.p0[:, 0:192], dd, T.oh[:]), ["dda", "ddb", "oh"], ["p0"])
        P(mm(T.p0[:, 192:384], dd, T.oh[:], True, False), ["dda", "ddb", "oh"], ["p0"])
        P(mm(T.p0[:, 192:384], T.cb[:], T.c255[:], False, True), ["cb", "c255"], ["p0"])
        use(4, 6)
        S(act(T.wn[:], T.p5[:, 0:192], AF.Relu, bias=-255.0, scale=-1.0), ["p5"], ["wn"])
        V(tt(T.f3[:], T.f2[:], T.p2[:, 192:384], A.add), ["f2", "p2"], ["f3"])
        V(ts(T.f4[:], T.f3[:], 4095, None, A.bitwise_and), ["f3"], ["f4"])
        V(tt(T.fd[:], T.f4[:], T.p2[:, 0:192], A.subtract), ["f4", "p2"], ["fd"])
        V(tt(T.si[:], T.wn[:], T.p6[:, 0:192], A.mult), ["wn", "p6"], ["si"])
        listmm("p5", 448, 12, "sel", "si", 192, ("b512",))
        V(cp(T.la[:], T.p6[:, 384:396]), ["p6"], ["la"])
        V(tt(T.zdb[:], T[z][:], T.p0[:, 0:192], A.subtract), [z, "p0"], ["zdb"])
        V(tt(T.yy[:], T.d0[:].indirect(T.la[:]), T.zdb[:], A.subtract), ["la", "zdb", "d0z"] + regs("d0", 0, 6), ["yy"])
        V(tt(T.xx[:], T.yy[:], T.p0[:, 192:384], A.max), ["yy", "p0"], ["xx"])
        if not lastt:
            S(act(T["zs%d" % (t + 1)][:], T.xx[:], AF.Abs), ["xx"], ["zs%d" % (t + 1)])
            send("zr%d" % (t + 1), "zs%d" % (t + 1), "zb%d" % (t + 1), 2 * t + 2)
        else:
            S(act(T.yzs[:], T.xx[:], AF.Abs), ["xx"], ["yzs"])
            op("s", lambda Q: Q.dma_start(T.yz[:], T.yzs[:]), ["yzs"], ["yz"], ("outz", 16, True))
        V(ts(T.p4[:, 192:384], T.p4[:, 0:192], 254.0, None, A.is_lt), ["p4"], ["p4", "ls"])
        V(tt(T.fw[:], T.fd[:], T.p4[:, 192:384], A.mult), ["ls", "fd", "p4"], ["fw"])
        V(ts(T.sl[:], T.p5[:, 448:460], 0.0625, None, A.mult), ["p5"], ["sl"])
        V(tt(T.tb[:].indirect(T.sl[:]), T.fw[:], T.of[:], A.add), ["fw", "of", "sl"], ["tb"])

    for t in range(STEPS):
        step(t)

    P(mm(T.p1[:, 0:256], T.cj[:], T.tb[:, 0:256]), ["cj", "tb"], ["p1"])
    P(mm(T.p2[:, 0:256], T.cj[:], T.tb[:, 256:512]), ["cj", "tb"], ["p2"])
    V(cp(T.yms[:, 0:256], T.p1[:, 0:256]), ["p1"], ["yma"])
    S(act(T.yms[:, 256:512], T.p2[:, 0:256], AF.Copy), ["p2"], ["ymb"])
    op("y", lambda Q: Q.dma_start(T.ymc[:, 0:256], T.yms[:, 0:256]), ["yma"], ["oa"], ("outa", 16, True))
    op("s", lambda Q: Q.dma_start(T.ymc[:, 256:512], T.yms[:, 256:512]), ["ymb"], ["ob"], ("outb", 16, True))
    emit()
    for s in ("outm", "outz", "outa", "outb"):
        g.wait_ge(T.sem[s], 16)
    g.wait_ge(T.sem.snd, n_eng * (2 * (STEPS - 1) + 1))
